import numpy as np
import ml_dtypes


def mxq(x, axis, fmt="e4m3"):
    dtype, down = {"e4m3": (ml_dtypes.float8_e4m3fn, 7), "e5m2": (ml_dtypes.float8_e5m2, 14)}[fmt]
    v = np.moveaxis(np.asarray(x, np.float32).astype(ml_dtypes.bfloat16).astype(np.float64), axis, -1)
    blocks = v.reshape(v.shape[:-1] + (-1, 32))
    amax = np.abs(blocks).max(-1, keepdims=True)
    byte = np.maximum(np.where(amax > 0, np.frexp(amax)[1] - 1 + 127, 0) - down, 1)
    scale = np.exp2(byte - 127.0)
    codes = (blocks / scale).astype(np.float32).astype(dtype).astype(np.float64)
    return np.moveaxis((codes * scale).reshape(v.shape), -1, axis)


WIDE = False


def mx_kscale(k):
    if not WIDE:
        return np.ones(k)
    levels = np.array([10, -10, 5, -5, 0])
    if k % 512:
        return np.exp2(np.random.permutation(np.resize(levels, k // 32))).repeat(32)
    a = np.empty((k // 512, 16))
    for p in range(k // 512):
        a[p, :8] = np.random.permutation(np.resize(levels, 8))
        for g in range(8):
            far = levels[np.abs(levels - a[p, g]) >= 10]
            a[p, g + 8] = far[np.random.randint(len(far))]
    return np.exp2(a.ravel()).repeat(32)


def f64(x):
    return np.asarray(x).astype(np.float64)


def striped(idx):
    return np.tile(idx.reshape(-1, 16).T, (8, 1)).astype(np.uint16)


def unstriped(offs):
    return offs[:16].T.reshape(-1).astype(np.int64)


def striped8(idx):
    return np.concatenate([x.reshape(-1, 16).T for x in idx]).astype(np.uint16)


def runs(offs, k):
    lists = np.stack([offs[16 * r : 16 * r + 16].T.reshape(-1) for r in range(8)]).astype(np.int64)
    return lists[np.arange(k) % 512 // 64]


def pack_weight(w):
    k, n = w.shape
    w = f64(np.asarray(w, np.float32).astype(ml_dtypes.bfloat16)).reshape(k // 32, 32, n)
    amax = np.abs(w).max(1)
    byte = np.clip(np.where(amax > 0, np.frexp(amax)[1] - 1 + 127 - 7, 1), 1, 254)
    scaled = (w * np.exp2(127.0 - byte)[:, None, :]).reshape(k, n).astype(np.float32)
    words = np.ascontiguousarray(scaled.reshape(k // 512, 128, 4, n).transpose(0, 1, 3, 2)).astype(ml_dtypes.float8_e4m3fn).view(np.uint8)
    return words, np.ascontiguousarray(byte.astype(np.uint8).reshape(k // 512, 16, n))


def unpack_weight(words, scales):
    g, p, n, _ = words.shape
    vals = np.ascontiguousarray(words).view(ml_dtypes.float8_e4m3fn).astype(np.float64) * np.repeat(np.exp2(scales.astype(np.float64) - 127.0), 8, axis=1)[..., None]
    return vals.transpose(0, 1, 3, 2).reshape(g * 512, n)


K, T, S, H, C = 512, 2048, 512, 512, 512


def setup_inputs():
    n = np.random.standard_normal
    s = mx_kscale(K)[:, None]
    packed_xT = pack_weight(n((K, T)) * s)
    return {
        "x_words": packed_xT[0],
        "x_scales": packed_xT[1],
        "w1": (n((K, H)) / np.sqrt(K) / s).astype(np.float32),
        "tau": np.random.uniform(0.3, 0.9, (H, 1)).astype(np.float32),
        "gs": (np.random.uniform(0.5, 1.5, (K, 1)) / s).astype(np.float32),
        "tau2": np.random.uniform(0.3, 0.9, (C, 1)).astype(np.float32),
        "offs": striped(np.random.permutation(T)[:S]),
        "n1": striped(np.random.permutation(S)),
        "n2": striped(np.random.permutation(S)),
        "ca": striped(np.random.permutation(T)[:C]),
        "hc": striped8(np.random.randint(0, T, (8, C))),
        "n3": striped8(np.stack([np.random.permutation(S) for _ in range(8)])),
        "n4": striped8(np.stack([np.random.permutation(S) for _ in range(8)])),
    }


def reference(x_words, x_scales, w1, tau, gs, tau2, offs, n1, n2, ca, hc, n3, n4):
    x_hc = unpack_weight(x_words, x_scales)[np.arange(K)[:, None], runs(hc, K)]
    xq = unpack_weight(x_words, x_scales)[:, unstriped(offs)]
    y = mxq(f64(w1), 0, "e4m3").T @ xq
    top = y.max(axis=1, keepdims=True)
    ea = np.exp(f64(tau) * (y[:, unstriped(n1)] - top))
    sm = y * ea
    ds = np.zeros((H, S))
    ds[:, unstriped(n2)] = sm
    z = f64(gs) * (2.0 * ds - (0.5 * y))
    zq = mxq(z, 0, "e4m3")
    b = 0.0625 * (x_hc.T @ zq)
    top2 = b.max(axis=1, keepdims=True)
    ea2 = np.exp(f64(tau2) * (b[np.arange(C)[:, None], runs(n3, C)] - top2))
    x_ca = unpack_weight(x_words, x_scales)[:, unstriped(ca)]
    a = 0.0625 * (x_ca.T @ zq)
    return (2.0 * ea2) * (a - (a[np.arange(C)[:, None], runs(n4, C)])) - (0.5 * b)

@@ -1,0 +1,205 @@
+import concourse.mybir as mybir
+
+K, T, S, H, C = 512, 2048, 512, 512, 512
+FLOPS = 2 * K * H * S + 2 * 2 * K * C * S
+
+F32 = mybir.dt.float32
+BF16 = mybir.dt.bfloat16
+I32 = mybir.dt.int32
+U32 = mybir.dt.uint32
+U16 = mybir.dt.uint16
+U8 = mybir.dt.uint8
+FP8X4 = mybir.dt.float8_e4m3fn_x4
+MULT = mybir.AluOpType.mult
+ADD = mybir.AluOpType.add
+SUB = mybir.AluOpType.subtract
+MAX = mybir.AluOpType.max
+COPY = mybir.ActivationFunctionType.Copy
+EXP = mybir.ActivationFunctionType.Exp
+
+P = 128
+PACK = 4
+HALF = S // 2
+LIST_COLS = S // 16
+HALVES = [(slice(h * HALF, (h + 1) * HALF), slice(h * LIST_COLS // 2, (h + 1) * LIST_COLS // 2)) for h in range(2)]
+VECTOR_CAST = 48
+
+
+def tile_picked_cdhpxbesd_none_p_kernel(
+    tc, x_words, x_scales, w1, tau, gs, tau2, offs, n1, n2, ca, hc, n3, n4, out
+):
+    nc = tc.nc
+    with (
+        tc.tile_pool(name="lists", bufs=1) as lists,
+        tc.tile_pool(name="keep", bufs=1) as keep,
+        tc.psum_pool(name="psum", bufs=1) as psum,
+    ):
+
+        def load_list(name, src):
+            tile = lists.tile([P, LIST_COLS], U16, name=name)
+            nc.sync.dma_start(tile[:], src)
+            return tile
+
+        def load_rows(name, src):
+            tile = keep.tile([P, PACK], F32, name=name)
+            nc.sync.dma_start(tile[:], src.rearrange("(p t) o -> p (t o)", t=PACK))
+            return tile
+
+        def mx(dst, lw, ls, rw, rs):
+            nc.tensor.matmul_mx(dst, lw.bitcast(FP8X4), ls, rw.bitcast(FP8X4), rs, start=True, stop=True)
+
+        x_bytes_q = keep.tile([P, T], U8, name="x_bytes_q", tag="codes_b", align_bytes=64)
+        nc.gpsimd.memset(x_bytes_q[:].bitcast(I32), 0)
+        x_bytes = keep.tile([P, T], U8, name="x_bytes", tag="window_bytes", align_bytes=64)
+        nc.gpsimd.memset(x_bytes[:].bitcast(I32), 0)
+        offs_t = load_list("offs_t", offs)
+        w_raw = keep.tile([P, PACK, H], F32, name="w_raw")
+        nc.sync.dma_start(w_raw[:], w1.rearrange("(p j) c -> p j c", j=PACK))
+        n1_t = load_list("n1_t", n1)
+        n2_t = load_list("n2_t", n2)
+        scale_rows = x_scales[0].rearrange("(q r) n -> r q n", r=4)
+        for r in range(4):
+            nc.sync.dma_start(x_bytes_q[r:P:32, :].bitcast(I32), scale_rows[r].bitcast(I32))
+        x_codes = keep.tile([P, T], U32, name="x_codes", tag="window_codes", align_bytes=64)
+        nc.sync.dma_start(x_codes[:].bitcast(I32), x_words[0].rearrange("p n t -> p (n t)").bitcast(I32))
+        tau_t = load_rows("tau_t", tau)
+        gs_t = load_rows("gs_t", gs)
+        ca_t = load_list("ca_t", ca)
+        hc_t = load_list("hc_t", hc)
+        n3_t = load_list("n3_t", n3)
+        n4_t = load_list("n4_t", n4)
+        tau2_t = load_rows("tau2_t", tau2)
+        for r in range(4):
+            nc.sync.dma_start(x_bytes[r:P:32, :].bitcast(I32), scale_rows[r].bitcast(I32))
+        for e in range(2):
+            nc.sync.dma_start(x_bytes[16 + e : P : 32, :].bitcast(I32), scale_rows[2 + e].bitcast(I32))
+
+        w_bf = keep.tile([P, PACK, P, PACK], BF16, name="w_bf", tag="codes_a", align_bytes=64)
+        w_dst = w_bf[:].rearrange("p t m j -> p m j t")
+        w_src = w_raw[:].rearrange("p j (m t) -> p m j t", t=PACK)
+        nc.scalar.activation(w_dst[:, VECTOR_CAST:], w_src[:, VECTOR_CAST:], COPY)
+        nc.vector.tensor_copy(w_dst[:, :VECTOR_CAST], w_src[:, :VECTOR_CAST])
+        q_bytes = keep.tile([P, S], U8, name="q_bytes", tag="bytes_a", align_bytes=64)
+        nc.vector.tensor_copy(q_bytes[:], x_bytes_q[:].indirect(offs_t[:]))
+        w_codes = keep.tile([P, H], U32, name="w_codes", tag="codes_b", align_bytes=64)
+        w_bytes = keep.tile([P, H], U8, name="w_bytes", tag="bytes_b", align_bytes=64)
+        nc.vector.quantize_mx(w_codes[:].bitcast(FP8X4), w_bytes[:], w_bf[:].rearrange("p t m j -> p (t m j)"))
+
+        q_codes = keep.tile([P, S], U32, name="q_codes", tag="codes_a", align_bytes=64)
+        y_ps = [psum.tile([P, S], F32, name="y_ps%d" % t, tag="ya%d" % t) for t in range(PACK)]
+        for cols, ent in HALVES:
+            nc.vector.tensor_copy(q_codes[:, cols], x_codes[:].indirect(offs_t[:, ent]))
+            mx(y_ps[0][:, cols], w_codes[:, 0:P], w_bytes[:, 0:P], q_codes[:, cols], q_bytes[:, cols])
+        for t in range(1, PACK):
+            m = slice(t * P, (t + 1) * P)
+            mx(y_ps[t][:], w_codes[:, m], w_bytes[:, m], q_codes[:], q_bytes[:])
+
+        gs_twice = keep.tile([P, PACK], F32, name="gs_twice")
+        gs_neg_half = keep.tile([P, PACK], F32, name="gs_neg_half")
+        nc.scalar.activation(gs_twice[:], gs_t[:], COPY, scale=2.0)
+        nc.scalar.activation(gs_neg_half[:], gs_t[:], COPY, scale=-0.5)
+
+        def window_and_bias(name, bank, factor, rate):
+            win = keep.tile([P, S], F32, name=name + "_win", tag=name + "_win")
+            top = keep.tile([P, 1], F32, name=name + "_top")
+            bias = keep.tile([P, 1], F32, name=name + "_bias")
+            nc.vector.tensor_scalar(win[:], bank[:], factor, None, MULT, MAX, accum_out=top[:])
+            nc.vector.tensor_scalar(bias[:], top[:], rate, -1.0, MULT, MULT)
+            return win, bias
+
+        z_codes = keep.tile([P, S], U32, name="z_codes", align_bytes=64)
+        z_bytes = keep.tile([P, S], U8, name="z_bytes", align_bytes=64)
+
+        def look_up(t, win, bias):
+            ea = keep.tile([P, S], F32, name="ea%d" % t)
+            sm = keep.tile([P, S], F32, name="sm%d" % t, tag="sm%d" % t)
+            for cols, ent in HALVES:
+                nc.scalar.activation(ea[:, cols], win[:].indirect(n1_t[:, ent]), EXP, bias=bias[:], scale=tau_t[:, t : t + 1])
+                nc.vector.scalar_tensor_tensor(sm[:, cols], y_ps[t][:, cols], gs_twice[:, t : t + 1], ea[:, cols], MULT, MULT)
+            return sm
+
+        def put_back(t, sm):
+            ds = keep.tile([P, S], F32, name="ds%d" % t, tag=("y2_win", "y3_win", "sm0", "sm1")[t])
+            cut = 128 if t == PACK - 1 else HALF
+            for lo, hi in ((0, cut), (cut, S)):
+                nc.scalar.activation(ds[:].indirect(n2_t[:, lo // 16 : hi // 16]), sm[:, lo:hi], COPY)
+            return ds
+
+        def make_z(t, ds, cols):
+            nc.vector.scalar_tensor_tensor(z_bf[:, cols, t], y_ps[t][:, cols], gs_neg_half[:, t : t + 1], ds[:, cols], MULT, ADD)
+
+        y_win = [window_and_bias("y%d" % t, y_ps[t], 1.0, tau_t[:, t : t + 1]) for t in range(2)]
+        sm0 = look_up(0, *y_win[0])
+        y_win.append(window_and_bias("y2", y_ps[2], 1.0, tau_t[:, 2:3]))
+        sm1 = look_up(1, *y_win[1])
+        y_win.append(window_and_bias("y3", y_ps[3], 1.0, tau_t[:, 3:4]))
+        sm2 = look_up(2, *y_win[2])
+        sm3 = look_up(3, *y_win[3])
+        ds0 = put_back(0, sm0)
+        ds1 = put_back(1, sm1)
+        ds2 = put_back(2, sm2)
+        ds3 = put_back(3, sm3)
+
+        h_bytes_raw = keep.tile([P, C], U8, name="h_bytes_raw", tag="bytes_a", align_bytes=64)
+        nc.vector.tensor_copy(h_bytes_raw[:], x_bytes[:].indirect(hc_t[:]))
+        h_bytes_dealt = keep.tile([P, C], U8, name="h_bytes_dealt", align_bytes=64)
+        nc.vector.tensor_copy(
+            h_bytes_dealt[:].rearrange("p (t m) -> p m t", t=PACK), h_bytes_raw[:].rearrange("p (m t) -> p m t", t=PACK)
+        )
+        h_bytes = keep.tile([P, C], U8, name="h_bytes", align_bytes=64)
+        nc.gpsimd.memset(h_bytes[:].bitcast(I32), 0)
+        for r, src in enumerate((0, 1, 16, 17)):
+            nc.sync.dma_start(h_bytes[r:P:32, :].bitcast(I32), h_bytes_dealt[src:P:32, :].bitcast(I32))
+
+        c_bytes = keep.tile([P, C], U8, name="c_bytes", tag="bytes_b", align_bytes=64)
+        nc.vector.tensor_copy(c_bytes[:].rearrange("p (t m) -> p m t", t=PACK), x_bytes[:].indirect(ca_t[:]))
+        h_codes_raw = keep.tile([P, C], U32, name="h_codes_raw", tag="window_bytes", align_bytes=64)
+        nc.vector.tensor_copy(h_codes_raw[:], x_codes[:].indirect(hc_t[:]))
+        h_codes = keep.tile([P, C], U32, name="h_codes", align_bytes=64)
+        nc.vector.tensor_copy(
+            h_codes[:].rearrange("p (t m) -> p m t", t=PACK), h_codes_raw[:].rearrange("p (m t) -> p m t", t=PACK)
+        )
+        c_codes = keep.tile([P, C], U32, name="c_codes", tag="codes_b", align_bytes=64)
+        nc.vector.tensor_copy(c_codes[:].rearrange("p (t m) -> p m t", t=PACK), x_codes[:].indirect(ca_t[:]))
+
+        z_bf = keep.tile([P, S, PACK], BF16, name="z_bf", tag="window_codes", align_bytes=64)
+        make_z(0, ds0, slice(0, S))
+        make_z(1, ds1, slice(0, S))
+        make_z(2, ds2, slice(0, S))
+        for cols, ent in HALVES:
+            make_z(3, ds3, cols)
+
+        b_ps = [psum.tile([P, S], F32, name="b_ps%d" % t, tag="b%d" % t) for t in range(PACK)]
+        a_ps = [psum.tile([P, S], F32, name="a_ps%d" % t, tag="ya%d" % t) for t in range(PACK)]
+        for cols, ent in HALVES:
+            nc.vector.quantize_mx(z_codes[:, cols].bitcast(FP8X4), z_bytes[:, cols], z_bf[:, cols, :].rearrange("p c t -> p (c t)"))
+            mx(a_ps[0][:, cols], c_codes[:, 0:P], c_bytes[:, 0:P], z_codes[:, cols], z_bytes[:, cols])
+            mx(b_ps[0][:, cols], h_codes[:, 0:P], h_bytes[:, 0:P], z_codes[:, cols], z_bytes[:, cols])
+        for t in range(1, PACK):
+            m = slice(t * P, (t + 1) * P)
+            mx(b_ps[t][:], h_codes[:, m], h_bytes[:, m], z_codes[:], z_bytes[:])
+            mx(a_ps[t][:], c_codes[:, m], c_bytes[:, m], z_codes[:], z_bytes[:])
+
+        out_rows = out.rearrange("(p t) n -> t p n", t=PACK)
+        b_win = [window_and_bias("b0", b_ps[0], 0.0625, tau2_t[:, 0:1])]
+        for t in range(PACK):
+            if t + 1 < PACK:
+                b_win.append(window_and_bias("b%d" % (t + 1), b_ps[t + 1], 0.0625, tau2_t[:, t + 1 : t + 2]))
+            win, bias = b_win[t]
+            a_win = keep.tile([P, S], F32, name="a_win%d" % t)
+            nc.scalar.activation(a_win[:], a_ps[t][:], COPY, scale=0.125)
+            for h, (cols, ent) in enumerate(HALVES):
+                looked = keep.tile([P, HALF], F32, name="looked%d_%d" % (t, h))
+                ea2 = keep.tile([P, HALF], F32, name="ea2_%d_%d" % (t, h))
+                diff = keep.tile([P, HALF], F32, name="diff%d_%d" % (t, h))
+                prod = keep.tile([P, HALF], F32, name="prod%d_%d" % (t, h))
+                res = keep.tile([P, HALF], F32, name="res%d_%d" % (t, h))
+                if (t, h) == (1, 1):
+                    nc.vector.tensor_copy(looked[:], a_win[:].indirect(n4_t[:, ent]))
+                else:
+                    nc.scalar.activation(looked[:], a_win[:].indirect(n4_t[:, ent]), COPY)
+                nc.scalar.activation(ea2[:], win[:].indirect(n3_t[:, ent]), EXP, bias=bias[:], scale=tau2_t[:, t : t + 1])
+                nc.vector.scalar_tensor_tensor(diff[:], a_ps[t][:, cols], 0.125, looked[:], MULT, SUB)
+                nc.vector.tensor_tensor(prod[:], diff[:], ea2[:], MULT)
+                nc.vector.scalar_tensor_tensor(res[:], b_ps[t][:, cols], -0.03125, prod[:], MULT, ADD)
+                nc.sync.dma_start(out_rows[t][:, cols], res[:])

@@ -86,25 +86,46 @@ def tile_picked_cdhpxbesd_none_p_kernel(
         nc.vector.quantize_mx(w_codes[:].bitcast(FP8X4), w_bytes[:], w_bf[:].rearrange("p t m j -> p (t m j)"))
 
         q_codes = keep.tile([P, S], U32, name="q_codes", tag="codes_a", align_bytes=64)
-        y_ps = [psum.tile([P, S], F32, name="y_ps%d" % t, tag="ya%d" % t) for t in range(PACK)]
-        for cols, ent in HALVES:
+        def bank(name, number, width=S):
+            return psum.tile([P, width], F32, name=name, tag="bank%d" % number)
+
+        def halves_of(tile):
+            return [tile[:, cols] for cols, ent in HALVES]
+
+        y_ps = [[bank("y_ps0_%d" % h, h, HALF)[:] for h in range(2)]]
+        for h, (cols, ent) in enumerate(HALVES):
             nc.vector.tensor_copy(q_codes[:, cols], x_codes[:].indirect(offs_t[:, ent]))
-            mx(y_ps[0][:, cols], w_codes[:, 0:P], w_bytes[:, 0:P], q_codes[:, cols], q_bytes[:, cols])
+            mx(y_ps[0][h], w_codes[:, 0:P], w_bytes[:, 0:P], q_codes[:, cols], q_bytes[:, cols])
+        y_banks = [None]
         for t in range(1, PACK):
             m = slice(t * P, (t + 1) * P)
-            mx(y_ps[t][:], w_codes[:, m], w_bytes[:, m], q_codes[:], q_bytes[:])
+            y_banks.append(bank("y_ps%d" % t, t + 1))
+            mx(y_banks[t][:], w_codes[:, m], w_bytes[:, m], q_codes[:], q_bytes[:])
+            y_ps.append(halves_of(y_banks[t]))
 
         gs_twice = keep.tile([P, PACK], F32, name="gs_twice")
         gs_neg_half = keep.tile([P, PACK], F32, name="gs_neg_half")
+        tau_neg = keep.tile([P, PACK], F32, name="tau_neg")
+        nc.scalar.activation(tau_neg[:], tau_t[:], COPY, scale=-1.0)
         nc.scalar.activation(gs_twice[:], gs_t[:], COPY, scale=2.0)
         nc.scalar.activation(gs_neg_half[:], gs_t[:], COPY, scale=-0.5)
 
         def window_and_bias(name, bank, factor, rate):
             win = keep.tile([P, S], F32, name=name + "_win", tag=name + "_win")
-            top = keep.tile([P, 1], F32, name=name + "_top")
+            top = keep.tile([P, 1], F32, name=name + "_top", tag=name + "_top")
             bias = keep.tile([P, 1], F32, name=name + "_bias")
             nc.vector.tensor_scalar(win[:], bank[:], factor, None, MULT, MAX, accum_out=top[:])
             nc.vector.tensor_scalar(bias[:], top[:], rate, -1.0, MULT, MULT)
+            return win, bias
+
+        def first_window_and_bias():
+            win = keep.tile([P, S], F32, name="y0_win", tag="y0_win")
+            top_half = keep.tile([P, 1], F32, name="y0_top_half", tag="y1_top")
+            top = keep.tile([P, 1], F32, name="y0_top")
+            bias = keep.tile([P, 1], F32, name="y0_bias")
+            nc.vector.tensor_scalar(win[:, 0:HALF], y_ps[0][0], 1.0, None, MULT, MAX, accum_out=top_half[:])
+            nc.vector.tensor_scalar(win[:, HALF:S], y_ps[0][1], 1.0, top_half[:], MULT, MAX, accum_out=top[:])
+            nc.scalar.activation(bias[:], top[:], COPY, scale=tau_neg[:, 0:1])
             return win, bias
 
         z_codes = keep.tile([P, S], U32, name="z_codes", align_bytes=64)
@@ -112,33 +133,37 @@ def tile_picked_cdhpxbesd_none_p_kernel(
 
         def look_up(t, win, bias):
             ea = keep.tile([P, S], F32, name="ea%d" % t)
-            sm = keep.tile([P, S], F32, name="sm%d" % t, tag="sm%d" % t)
             for cols, ent in HALVES:
                 nc.scalar.activation(ea[:, cols], win[:].indirect(n1_t[:, ent]), EXP, bias=bias[:], scale=tau_t[:, t : t + 1])
-                nc.vector.scalar_tensor_tensor(sm[:, cols], y_ps[t][:, cols], gs_twice[:, t : t + 1], ea[:, cols], MULT, MULT)
+            return ea
+
+        def weigh(t, ea):
+            sm = keep.tile([P, S], F32, name="sm%d" % t, tag="sm%d" % t)
+            for cols, y_part in y_parts[t]:
+                nc.vector.scalar_tensor_tensor(sm[:, cols], y_part, gs_twice[:, t : t + 1], ea[:, cols], MULT, MULT)
             return sm
 
         def put_back(t, sm):
-            ds = keep.tile([P, S], F32, name="ds%d" % t, tag=("y2_win", "y3_win", "sm0", "sm1")[t])
+            ds = keep.tile([P, S], F32, name="ds%d" % t, tag=("y1_win", "y2_win", "sm0", "sm1")[t])
             cut = 128 if t == PACK - 1 else HALF
             for lo, hi in ((0, cut), (cut, S)):
                 nc.scalar.activation(ds[:].indirect(n2_t[:, lo // 16 : hi // 16]), sm[:, lo:hi], COPY)
             return ds
 
-        def make_z(t, ds, cols):
-            nc.vector.scalar_tensor_tensor(z_bf[:, cols, t], y_ps[t][:, cols], gs_neg_half[:, t : t + 1], ds[:, cols], MULT, ADD)
+        def make_z(t, h):
+            cols, y_part = y_halves[t][h]
+            nc.vector.scalar_tensor_tensor(z_bf[h][:, :, t], y_part, gs_neg_half[:, t : t + 1], ds[t][:, cols], MULT, ADD)
 
-        y_win = [window_and_bias("y%d" % t, y_ps[t], 1.0, tau_t[:, t : t + 1]) for t in range(2)]
-        sm0 = look_up(0, *y_win[0])
-        y_win.append(window_and_bias("y2", y_ps[2], 1.0, tau_t[:, 2:3]))
-        sm1 = look_up(1, *y_win[1])
-        y_win.append(window_and_bias("y3", y_ps[3], 1.0, tau_t[:, 3:4]))
-        sm2 = look_up(2, *y_win[2])
-        sm3 = look_up(3, *y_win[3])
-        ds0 = put_back(0, sm0)
-        ds1 = put_back(1, sm1)
-        ds2 = put_back(2, sm2)
-        ds3 = put_back(3, sm3)
+        y_halves = [[(cols, y_ps[t][h]) for h, (cols, ent) in enumerate(HALVES)] for t in range(PACK)]
+        y_parts = [y_halves[0]] + [[(slice(0, S), y_banks[t][:])] for t in range(1, PACK)]
+        y_win = [first_window_and_bias()]
+        ea = []
+        for t in range(PACK):
+            if t + 1 < PACK:
+                y_win.append(window_and_bias("y%d" % (t + 1), y_banks[t + 1], 1.0, tau_t[:, t + 1 : t + 2]))
+            ea.append(look_up(t, *y_win[t]))
+        sm = [weigh(t, ea[t]) for t in range(PACK)]
+        ds = [put_back(t, sm[t]) for t in range(PACK)]
 
         h_bytes_raw = keep.tile([P, C], U8, name="h_bytes_raw", tag="bytes_a", align_bytes=64)
         nc.vector.tensor_copy(h_bytes_raw[:], x_bytes[:].indirect(hc_t[:]))
@@ -162,44 +187,74 @@ def tile_picked_cdhpxbesd_none_p_kernel(
         c_codes = keep.tile([P, C], U32, name="c_codes", tag="codes_b", align_bytes=64)
         nc.vector.tensor_copy(c_codes[:].rearrange("p (t m) -> p m t", t=PACK), x_codes[:].indirect(ca_t[:]))
 
-        z_bf = keep.tile([P, S, PACK], BF16, name="z_bf", tag="window_codes", align_bytes=64)
-        make_z(0, ds0, slice(0, S))
-        make_z(1, ds1, slice(0, S))
-        make_z(2, ds2, slice(0, S))
-        for cols, ent in HALVES:
-            make_z(3, ds3, cols)
+        z_bf = [
+            keep.tile([P, HALF, PACK], BF16, name="z_bf%d" % h, tag=("window_codes", "window_bytes")[h], align_bytes=64)
+            for h in range(2)
+        ]
+        for t in range(PACK - 1):
+            for h in (1, 0):
+                make_z(t, h)
+        y_term = keep.tile([P, HALF], F32, name="y_term", tag="sm0")
+        nc.vector.tensor_scalar(y_term[:], y_halves[3][1][1], gs_neg_half[:, 3:4], None, MULT)
+        nc.gpsimd.tensor_tensor(z_bf[1][:, :, 3], ds[3][:, HALF:S], y_term[:], ADD)
+        make_z(3, 0)
 
-        b_ps = [psum.tile([P, S], F32, name="b_ps%d" % t, tag="b%d" % t) for t in range(PACK)]
-        a_ps = [psum.tile([P, S], F32, name="a_ps%d" % t, tag="ya%d" % t) for t in range(PACK)]
-        for cols, ent in HALVES:
-            nc.vector.quantize_mx(z_codes[:, cols].bitcast(FP8X4), z_bytes[:, cols], z_bf[:, cols, :].rearrange("p c t -> p (c t)"))
-            mx(a_ps[0][:, cols], c_codes[:, 0:P], c_bytes[:, 0:P], z_codes[:, cols], z_bytes[:, cols])
-            mx(b_ps[0][:, cols], h_codes[:, 0:P], h_bytes[:, 0:P], z_codes[:, cols], z_bytes[:, cols])
+        a_ps = [[bank("a_ps0_%d" % h, 5 + h, HALF)[:] for h in range(2)]]
+        b_banks = [bank("b_ps0", 7)]
+        for h, (cols, ent) in enumerate(HALVES):
+            nc.vector.quantize_mx(z_codes[:, cols].bitcast(FP8X4), z_bytes[:, cols], z_bf[h][:].rearrange("p c t -> p (c t)"))
+            mx(a_ps[0][h], c_codes[:, 0:P], c_bytes[:, 0:P], z_codes[:, cols], z_bytes[:, cols])
+            mx(b_banks[0][:, cols], h_codes[:, 0:P], h_bytes[:, 0:P], z_codes[:, cols], z_bytes[:, cols])
+        a_banks = [None]
         for t in range(1, PACK):
             m = slice(t * P, (t + 1) * P)
-            mx(b_ps[t][:], h_codes[:, m], h_bytes[:, m], z_codes[:], z_bytes[:])
-            mx(a_ps[t][:], c_codes[:, m], c_bytes[:, m], z_codes[:], z_bytes[:])
+            a_banks.append(bank("a_ps%d" % t, 2 * t - 2))
+            mx(a_banks[t][:], c_codes[:, m], c_bytes[:, m], z_codes[:], z_bytes[:])
+            a_ps.append(halves_of(a_banks[t]))
+            b_banks.append(bank("b_ps%d" % t, 2 * t - 1))
+            mx(b_banks[t][:], h_codes[:, m], h_bytes[:, m], z_codes[:], z_bytes[:])
 
         out_rows = out.rearrange("(p t) n -> t p n", t=PACK)
-        b_win = [window_and_bias("b0", b_ps[0], 0.0625, tau2_t[:, 0:1])]
-        for t in range(PACK):
-            if t + 1 < PACK:
-                b_win.append(window_and_bias("b%d" % (t + 1), b_ps[t + 1], 0.0625, tau2_t[:, t + 1 : t + 2]))
-            win, bias = b_win[t]
+        a_halves = [[(cols, a_ps[t][h]) for h, (cols, ent) in enumerate(HALVES)] for t in range(PACK)]
+        a_parts = [a_halves[0]] + [[(slice(0, S), a_banks[t][:])] for t in range(1, PACK)]
+
+        def windows(t):
             a_win = keep.tile([P, S], F32, name="a_win%d" % t)
-            nc.scalar.activation(a_win[:], a_ps[t][:], COPY, scale=0.125)
+            for cols, a_part in a_parts[t]:
+                nc.scalar.activation(a_win[:, cols], a_part, COPY, scale=0.125)
+            return (a_win,) + window_and_bias("b%d" % t, b_banks[t], 0.0625, tau2_t[:, t : t + 1])
+
+        def finish(t, prod, cols):
+            res = keep.tile([P, S], F32, name="res%d_%d" % (t, cols.start))
+            nc.vector.scalar_tensor_tensor(res[:, cols], b_banks[t][:, cols], -0.03125, prod[:, cols], MULT, ADD)
+            nc.sync.dma_start(out_rows[t][:, cols], res[:, cols])
+
+        ready = [windows(0), windows(1)]
+        prods = []
+        for t in range(PACK):
+            last = t == PACK - 1
+            a_win, b_win, bias = ready[t]
+            looked = keep.tile([P, S], F32, name="looked%d" % t)
+            diff = keep.tile([P, S], F32, name="diff%d" % t)
+            ea2 = keep.tile([P, S], F32, name="ea2_%d" % t)
+            prod = keep.tile([P, S], F32, name="prod%d" % t)
             for h, (cols, ent) in enumerate(HALVES):
-                looked = keep.tile([P, HALF], F32, name="looked%d_%d" % (t, h))
-                ea2 = keep.tile([P, HALF], F32, name="ea2_%d_%d" % (t, h))
-                diff = keep.tile([P, HALF], F32, name="diff%d_%d" % (t, h))
-                prod = keep.tile([P, HALF], F32, name="prod%d_%d" % (t, h))
-                res = keep.tile([P, HALF], F32, name="res%d_%d" % (t, h))
-                if (t, h) == (1, 1):
-                    nc.vector.tensor_copy(looked[:], a_win[:].indirect(n4_t[:, ent]))
+                if h == 1 and t < 2:
+                    nc.vector.tensor_copy(looked[:, cols], a_win[:].indirect(n4_t[:, ent]))
                 else:
-                    nc.scalar.activation(looked[:], a_win[:].indirect(n4_t[:, ent]), COPY)
-                nc.scalar.activation(ea2[:], win[:].indirect(n3_t[:, ent]), EXP, bias=bias[:], scale=tau2_t[:, t : t + 1])
-                nc.vector.scalar_tensor_tensor(diff[:], a_ps[t][:, cols], 0.125, looked[:], MULT, SUB)
+                    nc.scalar.activation(looked[:, cols], a_win[:].indirect(n4_t[:, ent]), COPY)
+            for cols, a_part in a_halves[t] if last else a_parts[t]:
+                nc.vector.scalar_tensor_tensor(diff[:, cols], a_part, 0.125, looked[:, cols], MULT, SUB)
+            for cols, ent in HALVES:
+                nc.scalar.activation(ea2[:, cols], b_win[:].indirect(n3_t[:, ent]), EXP, bias=bias[:], scale=tau2_t[:, t : t + 1])
+            if t > 0:
+                finish(t - 1, prods[t - 1], slice(0, S))
+            if last:
+                for cols, ent in HALVES:
+                    nc.vector.tensor_tensor(prod[:, cols], diff[:, cols], ea2[:, cols], MULT)
+                    finish(t, prod, cols)
+            else:
                 nc.vector.tensor_tensor(prod[:], diff[:], ea2[:], MULT)
-                nc.vector.scalar_tensor_tensor(res[:], b_ps[t][:, cols], -0.03125, prod[:], MULT, ADD)
-                nc.sync.dma_start(out_rows[t][:, cols], res[:])
+                prods.append(prod)
+            if t + 2 < PACK:
+                ready.append(windows(t + 2))

@@ -105,8 +105,10 @@ def tile_picked_cdhpxbesd_none_p_kernel(
 
         gs_twice = keep.tile([P, PACK], F32, name="gs_twice")
         gs_neg_half = keep.tile([P, PACK], F32, name="gs_neg_half")
-        tau_neg = keep.tile([P, PACK], F32, name="tau_neg")
-        nc.scalar.activation(tau_neg[:], tau_t[:], COPY, scale=-1.0)
+        tau_neg = keep.tile([P, 1], F32, name="tau_neg")
+        nc.scalar.activation(tau_neg[:], tau_t[:, 0:1], COPY, scale=-1.0)
+        tau2_neg = keep.tile([P, 1], F32, name="tau2_neg")
+        nc.gpsimd.tensor_scalar(tau2_neg[:], tau2_t[:, 0:1], -1.0, 0.0, MULT, ADD)
         nc.scalar.activation(gs_twice[:], gs_t[:], COPY, scale=2.0)
         nc.scalar.activation(gs_neg_half[:], gs_t[:], COPY, scale=-0.5)
 
@@ -115,17 +117,16 @@ def tile_picked_cdhpxbesd_none_p_kernel(
             top = keep.tile([P, 1], F32, name=name + "_top", tag=name + "_top")
             bias = keep.tile([P, 1], F32, name=name + "_bias")
             nc.vector.tensor_scalar(win[:], bank[:], factor, None, MULT, MAX, accum_out=top[:])
-            nc.vector.tensor_scalar(bias[:], top[:], rate, -1.0, MULT, MULT)
+            nc.gpsimd.tensor_scalar(bias[:], top[:], rate, -1.0, MULT, MULT)
             return win, bias
 
         def first_window_and_bias():
             win = keep.tile([P, S], F32, name="y0_win", tag="y0_win")
-            top_half = keep.tile([P, 1], F32, name="y0_top_half", tag="y1_top")
-            top = keep.tile([P, 1], F32, name="y0_top")
+            tops = keep.tile([P, 2], F32, name="y0_top")
             bias = keep.tile([P, 1], F32, name="y0_bias")
-            nc.vector.tensor_scalar(win[:, 0:HALF], y_ps[0][0], 1.0, None, MULT, MAX, accum_out=top_half[:])
-            nc.vector.tensor_scalar(win[:, HALF:S], y_ps[0][1], 1.0, top_half[:], MULT, MAX, accum_out=top[:])
-            nc.scalar.activation(bias[:], top[:], COPY, scale=tau_neg[:, 0:1])
+            for h, (cols, ent) in enumerate(HALVES):
+                nc.vector.tensor_scalar(win[:, cols], y_ps[0][h], 1.0, None, MULT, MAX, accum_out=tops[:, h : h + 1])
+            nc.gpsimd.tensor_scalar(bias[:], tops[:, 0:1], tops[:, 1:2], tau_neg[:, 0:1], MAX, MULT)
             return win, bias
 
         z_codes = keep.tile([P, S], U32, name="z_codes", align_bytes=64)
@@ -144,7 +145,7 @@ def tile_picked_cdhpxbesd_none_p_kernel(
             return sm
 
         def put_back(t, sm):
-            ds = keep.tile([P, S], F32, name="ds%d" % t, tag=("y1_win", "y2_win", "sm0", "sm1")[t])
+            ds = keep.tile([P, S], F32, name="ds%d" % t, tag=("y2_win", "y3_win", "sm0", "sm1")[t])
             cut = 128 if t == PACK - 1 else HALF
             for lo, hi in ((0, cut), (cut, S)):
                 nc.scalar.activation(ds[:].indirect(n2_t[:, lo // 16 : hi // 16]), sm[:, lo:hi], COPY)
@@ -199,62 +200,75 @@ def tile_picked_cdhpxbesd_none_p_kernel(
         nc.gpsimd.tensor_tensor(z_bf[1][:, :, 3], ds[3][:, HALF:S], y_term[:], ADD)
         make_z(3, 0)
 
-        a_ps = [[bank("a_ps0_%d" % h, 5 + h, HALF)[:] for h in range(2)]]
-        b_banks = [bank("b_ps0", 7)]
+        a_first = [bank("a_ps0_%d" % h, 5 + h, HALF)[:] for h in range(2)]
+        b_first = [bank("b_ps0_%d" % h, (7 + h) % 8, HALF)[:] for h in range(2)]
         for h, (cols, ent) in enumerate(HALVES):
             nc.vector.quantize_mx(z_codes[:, cols].bitcast(FP8X4), z_bytes[:, cols], z_bf[h][:].rearrange("p c t -> p (c t)"))
-            mx(a_ps[0][h], c_codes[:, 0:P], c_bytes[:, 0:P], z_codes[:, cols], z_bytes[:, cols])
-            mx(b_banks[0][:, cols], h_codes[:, 0:P], h_bytes[:, 0:P], z_codes[:, cols], z_bytes[:, cols])
-        a_banks = [None]
+            mx(a_first[h], c_codes[:, 0:P], c_bytes[:, 0:P], z_codes[:, cols], z_bytes[:, cols])
+            mx(b_first[h], h_codes[:, 0:P], h_bytes[:, 0:P], z_codes[:, cols], z_bytes[:, cols])
+        a_banks, b_banks = [None], [None]
         for t in range(1, PACK):
             m = slice(t * P, (t + 1) * P)
-            a_banks.append(bank("a_ps%d" % t, 2 * t - 2))
+            a_banks.append(bank("a_ps%d" % t, 2 * t - 1))
             mx(a_banks[t][:], c_codes[:, m], c_bytes[:, m], z_codes[:], z_bytes[:])
-            a_ps.append(halves_of(a_banks[t]))
-            b_banks.append(bank("b_ps%d" % t, 2 * t - 1))
+            b_banks.append(bank("b_ps%d" % t, 2 * t))
             mx(b_banks[t][:], h_codes[:, m], h_bytes[:, m], z_codes[:], z_bytes[:])
 
         out_rows = out.rearrange("(p t) n -> t p n", t=PACK)
-        a_halves = [[(cols, a_ps[t][h]) for h, (cols, ent) in enumerate(HALVES)] for t in range(PACK)]
-        a_parts = [a_halves[0]] + [[(slice(0, S), a_banks[t][:])] for t in range(1, PACK)]
+        half_cols = [cols for cols, ent in HALVES]
+        whole = slice(0, S)
+        a_parts = [list(zip(half_cols, a_first))] + [[(whole, a_banks[t][:])] for t in range(1, PACK - 1)]
+        b_parts = [list(zip(half_cols, b_first))] + [[(whole, b_banks[t][:])] for t in range(1, PACK - 1)]
+        a_parts.append(list(zip(half_cols, halves_of(a_banks[PACK - 1]))))
+        b_parts.append(list(zip(half_cols, halves_of(b_banks[PACK - 1]))))
+
+        def first_windows():
+            a_win = keep.tile([P, S], F32, name="a_win0")
+            b_win = keep.tile([P, S], F32, name="b0_win")
+            tops = keep.tile([P, 2], F32, name="b0_top", tag="b0_top")
+            bias = keep.tile([P, 1], F32, name="b0_bias")
+            for cols, a_part in a_parts[0]:
+                nc.scalar.activation(a_win[:, cols], a_part, COPY, scale=0.125)
+            for h, (cols, b_part) in enumerate(b_parts[0]):
+                nc.vector.tensor_scalar(b_win[:, cols], b_part, 0.0625, None, MULT, MAX, accum_out=tops[:, h : h + 1])
+            nc.gpsimd.tensor_scalar(bias[:], tops[:, 0:1], tops[:, 1:2], tau2_neg[:], MAX, MULT)
+            return a_win, b_win, bias
 
         def windows(t):
             a_win = keep.tile([P, S], F32, name="a_win%d" % t)
-            for cols, a_part in a_parts[t]:
-                nc.scalar.activation(a_win[:, cols], a_part, COPY, scale=0.125)
+            nc.vector.tensor_scalar(a_win[:], a_banks[t][:], 0.125, None, MULT)
             return (a_win,) + window_and_bias("b%d" % t, b_banks[t], 0.0625, tau2_t[:, t : t + 1])
 
-        def finish(t, prod, cols):
-            res = keep.tile([P, S], F32, name="res%d_%d" % (t, cols.start))
-            nc.vector.scalar_tensor_tensor(res[:, cols], b_banks[t][:, cols], -0.03125, prod[:, cols], MULT, ADD)
-            nc.sync.dma_start(out_rows[t][:, cols], res[:, cols])
+        def finish(t, prod):
+            res = keep.tile([P, S], F32, name="res%d" % t)
+            for cols, b_part in b_parts[t]:
+                nc.vector.scalar_tensor_tensor(res[:, cols], b_part, -0.03125, prod[:, cols], MULT, ADD)
+            nc.sync.dma_start(out_rows[t], res[:])
 
-        ready = [windows(0), windows(1)]
+        ready = [first_windows(), windows(1)]
         prods = []
         for t in range(PACK):
-            last = t == PACK - 1
             a_win, b_win, bias = ready[t]
             looked = keep.tile([P, S], F32, name="looked%d" % t)
             diff = keep.tile([P, S], F32, name="diff%d" % t)
             ea2 = keep.tile([P, S], F32, name="ea2_%d" % t)
-            prod = keep.tile([P, S], F32, name="prod%d" % t)
-            for h, (cols, ent) in enumerate(HALVES):
-                if h == 1 and t < 2:
-                    nc.vector.tensor_copy(looked[:, cols], a_win[:].indirect(n4_t[:, ent]))
-                else:
-                    nc.scalar.activation(looked[:, cols], a_win[:].indirect(n4_t[:, ent]), COPY)
-            for cols, a_part in a_halves[t] if last else a_parts[t]:
+            for cols, ent in HALVES:
+                nc.scalar.activation(looked[:, cols], a_win[:].indirect(n4_t[:, ent]), COPY)
+            for cols, a_part in a_parts[t]:
                 nc.vector.scalar_tensor_tensor(diff[:, cols], a_part, 0.125, looked[:, cols], MULT, SUB)
             for cols, ent in HALVES:
                 nc.scalar.activation(ea2[:, cols], b_win[:].indirect(n3_t[:, ent]), EXP, bias=bias[:], scale=tau2_t[:, t : t + 1])
             if t > 0:
-                finish(t - 1, prods[t - 1], slice(0, S))
-            if last:
-                for cols, ent in HALVES:
-                    nc.vector.tensor_tensor(prod[:, cols], diff[:, cols], ea2[:, cols], MULT)
-                    finish(t, prod, cols)
-            else:
-                nc.vector.tensor_tensor(prod[:], diff[:], ea2[:], MULT)
+                finish(t - 1, prods[t - 1])
+            prod = keep.tile([P, S], F32, name="prod%d" % t, tag="prod%d" % min(t, PACK - 2))
+            if t + 1 < PACK:
+                nc.gpsimd.tensor_tensor(prod[:], diff[:], ea2[:], MULT)
                 prods.append(prod)
+            else:
+                res = keep.tile([P, S], F32, name="res%d" % t)
+                for cols, b_part in b_parts[t]:
+                    nc.vector.tensor_tensor(prod[:, cols], diff[:, cols], ea2[:, cols], MULT)
+                    nc.vector.scalar_tensor_tensor(res[:, cols], b_part, -0.03125, prod[:, cols], MULT, ADD)
+                    nc.sync.dma_start(out_rows[t][:, cols], res[:, cols])
             if t + 2 < PACK:
                 ready.append(windows(t + 2))

@@ -195,9 +195,9 @@ def tile_picked_cdhpxbesd_none_p_kernel(
         for t in range(PACK - 1):
             for h in (1, 0):
                 make_z(t, h)
-        y_term = keep.tile([P, HALF], F32, name="y_term", tag="sm0")
-        nc.vector.tensor_scalar(y_term[:], y_halves[3][1][1], gs_neg_half[:, 3:4], None, MULT)
-        nc.gpsimd.tensor_tensor(z_bf[1][:, :, 3], ds[3][:, HALF:S], y_term[:], ADD)
+        z_flat = keep.tile([P, HALF], BF16, name="z_flat", tag="sm0")
+        nc.vector.scalar_tensor_tensor(z_flat[:], y_halves[3][1][1], gs_neg_half[:, 3:4], ds[3][:, HALF:S], MULT, ADD)
+        nc.scalar.copy(z_bf[1][:, :, 3], z_flat[:])
         make_z(3, 0)
 
         a_first = [bank("a_ps0_%d" % h, 5 + h, HALF)[:] for h in range(2)]
@@ -260,9 +260,9 @@ def tile_picked_cdhpxbesd_none_p_kernel(
                 nc.scalar.activation(ea2[:, cols], b_win[:].indirect(n3_t[:, ent]), EXP, bias=bias[:], scale=tau2_t[:, t : t + 1])
             if t > 0:
                 finish(t - 1, prods[t - 1])
-            prod = keep.tile([P, S], F32, name="prod%d" % t, tag="prod%d" % min(t, PACK - 2))
+            prod = keep.tile([P, S], F32, name="prod%d" % t)
             if t + 1 < PACK:
-                nc.gpsimd.tensor_tensor(prod[:], diff[:], ea2[:], MULT)
+                (nc.gpsimd if t < 2 else nc.vector).tensor_tensor(prod[:], diff[:], ea2[:], MULT)
                 prods.append(prod)
             else:
                 res = keep.tile([P, S], F32, name="res%d" % t)

import concourse.mybir as mybir

K, T, S, H, C = 512, 2048, 512, 512, 512
FLOPS = 2 * K * H * S + 2 * 2 * K * C * S

F32 = mybir.dt.float32
BF16 = mybir.dt.bfloat16
I32 = mybir.dt.int32
U32 = mybir.dt.uint32
U16 = mybir.dt.uint16
U8 = mybir.dt.uint8
FP8X4 = mybir.dt.float8_e4m3fn_x4
MULT = mybir.AluOpType.mult
ADD = mybir.AluOpType.add
SUB = mybir.AluOpType.subtract
MAX = mybir.AluOpType.max
COPY = mybir.ActivationFunctionType.Copy
EXP = mybir.ActivationFunctionType.Exp

P = 128
PACK = 4
HALF = S // 2
LIST_COLS = S // 16
HALVES = [(slice(h * HALF, (h + 1) * HALF), slice(h * LIST_COLS // 2, (h + 1) * LIST_COLS // 2)) for h in range(2)]
VECTOR_CAST = 48


def tile_picked_cdhpxbesd_none_p_kernel(
    tc, x_words, x_scales, w1, tau, gs, tau2, offs, n1, n2, ca, hc, n3, n4, out
):
    nc = tc.nc
    with (
        tc.tile_pool(name="lists", bufs=1) as lists,
        tc.tile_pool(name="keep", bufs=1) as keep,
        tc.psum_pool(name="psum", bufs=1) as psum,
    ):

        def load_list(name, src):
            tile = lists.tile([P, LIST_COLS], U16, name=name)
            nc.sync.dma_start(tile[:], src)
            return tile

        def load_rows(name, src):
            tile = keep.tile([P, PACK], F32, name=name)
            nc.sync.dma_start(tile[:], src.rearrange("(p t) o -> p (t o)", t=PACK))
            return tile

        def mx(dst, lw, ls, rw, rs):
            nc.tensor.matmul_mx(dst, lw.bitcast(FP8X4), ls, rw.bitcast(FP8X4), rs, start=True, stop=True)

        x_bytes_q = keep.tile([P, T], U8, name="x_bytes_q", tag="codes_b", align_bytes=64)
        nc.gpsimd.memset(x_bytes_q[:].bitcast(I32), 0)
        x_bytes = keep.tile([P, T], U8, name="x_bytes", tag="window_bytes", align_bytes=64)
        nc.gpsimd.memset(x_bytes[:].bitcast(I32), 0)
        offs_t = load_list("offs_t", offs)
        w_raw = keep.tile([P, PACK, H], F32, name="w_raw")
        nc.sync.dma_start(w_raw[:], w1.rearrange("(p j) c -> p j c", j=PACK))
        n1_t = load_list("n1_t", n1)
        n2_t = load_list("n2_t", n2)
        scale_rows = x_scales[0].rearrange("(q r) n -> r q n", r=4)
        for r in range(4):
            nc.sync.dma_start(x_bytes_q[r:P:32, :].bitcast(I32), scale_rows[r].bitcast(I32))
        x_codes = keep.tile([P, T], U32, name="x_codes", tag="window_codes", align_bytes=64)
        nc.sync.dma_start(x_codes[:].bitcast(I32), x_words[0].rearrange("p n t -> p (n t)").bitcast(I32))
        tau_t = load_rows("tau_t", tau)
        gs_t = load_rows("gs_t", gs)
        ca_t = load_list("ca_t", ca)
        hc_t = load_list("hc_t", hc)
        n3_t = load_list("n3_t", n3)
        n4_t = load_list("n4_t", n4)
        tau2_t = load_rows("tau2_t", tau2)
        for r in range(4):
            nc.sync.dma_start(x_bytes[r:P:32, :].bitcast(I32), scale_rows[r].bitcast(I32))
        for e in range(2):
            nc.sync.dma_start(x_bytes[16 + e : P : 32, :].bitcast(I32), scale_rows[2 + e].bitcast(I32))

        w_bf = keep.tile([P, PACK, P, PACK], BF16, name="w_bf", tag="codes_a", align_bytes=64)
        w_dst = w_bf[:].rearrange("p t m j -> p m j t")
        w_src = w_raw[:].rearrange("p j (m t) -> p m j t", t=PACK)
        nc.scalar.activation(w_dst[:, VECTOR_CAST:], w_src[:, VECTOR_CAST:], COPY)
        nc.vector.tensor_copy(w_dst[:, :VECTOR_CAST], w_src[:, :VECTOR_CAST])
        q_bytes = keep.tile([P, S], U8, name="q_bytes", tag="bytes_a", align_bytes=64)
        nc.vector.tensor_copy(q_bytes[:], x_bytes_q[:].indirect(offs_t[:]))
        w_codes = keep.tile([P, H], U32, name="w_codes", tag="codes_b", align_bytes=64)
        w_bytes = keep.tile([P, H], U8, name="w_bytes", tag="bytes_b", align_bytes=64)
        nc.vector.quantize_mx(w_codes[:].bitcast(FP8X4), w_bytes[:], w_bf[:].rearrange("p t m j -> p (t m j)"))

        q_codes = keep.tile([P, S], U32, name="q_codes", tag="codes_a", align_bytes=64)
        def bank(name, number, width=S):
            return psum.tile([P, width], F32, name=name, tag="bank%d" % number)

        def halves_of(tile):
            return [tile[:, cols] for cols, ent in HALVES]

        y_ps = [[bank("y_ps0_%d" % h, h, HALF)[:] for h in range(2)]]
        for h, (cols, ent) in enumerate(HALVES):
            nc.vector.tensor_copy(q_codes[:, cols], x_codes[:].indirect(offs_t[:, ent]))
            mx(y_ps[0][h], w_codes[:, 0:P], w_bytes[:, 0:P], q_codes[:, cols], q_bytes[:, cols])
        y_banks = [None]
        for t in range(1, PACK):
            m = slice(t * P, (t + 1) * P)
            y_banks.append(bank("y_ps%d" % t, t + 1))
            mx(y_banks[t][:], w_codes[:, m], w_bytes[:, m], q_codes[:], q_bytes[:])
            y_ps.append(halves_of(y_banks[t]))

        gs_twice = keep.tile([P, PACK], F32, name="gs_twice")
        gs_neg_half = keep.tile([P, PACK], F32, name="gs_neg_half")
        tau_neg = keep.tile([P, 1], F32, name="tau_neg")
        nc.scalar.activation(tau_neg[:], tau_t[:, 0:1], COPY, scale=-1.0)
        tau2_neg = keep.tile([P, 1], F32, name="tau2_neg")
        nc.gpsimd.tensor_scalar(tau2_neg[:], tau2_t[:, 0:1], -1.0, 0.0, MULT, ADD)
        nc.scalar.activation(gs_twice[:], gs_t[:], COPY, scale=2.0)
        nc.scalar.activation(gs_neg_half[:], gs_t[:], COPY, scale=-0.5)

        def window_and_bias(name, bank, factor, rate):
            win = keep.tile([P, S], F32, name=name + "_win", tag=name + "_win")
            top = keep.tile([P, 1], F32, name=name + "_top", tag=name + "_top")
            bias = keep.tile([P, 1], F32, name=name + "_bias")
            nc.vector.tensor_scalar(win[:], bank[:], factor, None, MULT, MAX, accum_out=top[:])
            nc.gpsimd.tensor_scalar(bias[:], top[:], rate, -1.0, MULT, MULT)
            return win, bias

        def first_window_and_bias():
            win = keep.tile([P, S], F32, name="y0_win", tag="y0_win")
            tops = keep.tile([P, 2], F32, name="y0_top")
            bias = keep.tile([P, 1], F32, name="y0_bias")
            for h, (cols, ent) in enumerate(HALVES):
                nc.vector.tensor_scalar(win[:, cols], y_ps[0][h], 1.0, None, MULT, MAX, accum_out=tops[:, h : h + 1])
            nc.gpsimd.tensor_scalar(bias[:], tops[:, 0:1], tops[:, 1:2], tau_neg[:, 0:1], MAX, MULT)
            return win, bias

        z_codes = keep.tile([P, S], U32, name="z_codes", align_bytes=64)
        z_bytes = keep.tile([P, S], U8, name="z_bytes", align_bytes=64)

        def look_up(t, win, bias):
            ea = keep.tile([P, S], F32, name="ea%d" % t)
            for cols, ent in HALVES:
                nc.scalar.activation(ea[:, cols], win[:].indirect(n1_t[:, ent]), EXP, bias=bias[:], scale=tau_t[:, t : t + 1])
            return ea

        def weigh(t, ea):
            sm = keep.tile([P, S], F32, name="sm%d" % t, tag="sm%d" % t)
            for cols, y_part in y_parts[t]:
                nc.vector.scalar_tensor_tensor(sm[:, cols], y_part, gs_twice[:, t : t + 1], ea[:, cols], MULT, MULT)
            return sm

        def put_back(t, sm):
            ds = keep.tile([P, S], F32, name="ds%d" % t, tag=("y2_win", "y3_win", "sm0", "sm1")[t])
            cut = 128 if t == PACK - 1 else HALF
            for lo, hi in ((0, cut), (cut, S)):
                nc.scalar.activation(ds[:].indirect(n2_t[:, lo // 16 : hi // 16]), sm[:, lo:hi], COPY)
            return ds

        def make_z(t, h):
            cols, y_part = y_halves[t][h]
            nc.vector.scalar_tensor_tensor(z_bf[h][:, :, t], y_part, gs_neg_half[:, t : t + 1], ds[t][:, cols], MULT, ADD)

        y_halves = [[(cols, y_ps[t][h]) for h, (cols, ent) in enumerate(HALVES)] for t in range(PACK)]
        y_parts = [y_halves[0]] + [[(slice(0, S), y_banks[t][:])] for t in range(1, PACK)]
        y_win = [first_window_and_bias()]
        ea = []
        for t in range(PACK):
            if t + 1 < PACK:
                y_win.append(window_and_bias("y%d" % (t + 1), y_banks[t + 1], 1.0, tau_t[:, t + 1 : t + 2]))
            ea.append(look_up(t, *y_win[t]))
        sm = [weigh(t, ea[t]) for t in range(PACK)]
        ds = [put_back(t, sm[t]) for t in range(PACK)]

        h_bytes_raw = keep.tile([P, C], U8, name="h_bytes_raw", tag="bytes_a", align_bytes=64)
        nc.vector.tensor_copy(h_bytes_raw[:], x_bytes[:].indirect(hc_t[:]))
        h_bytes_dealt = keep.tile([P, C], U8, name="h_bytes_dealt", align_bytes=64)
        nc.vector.tensor_copy(
            h_bytes_dealt[:].rearrange("p (t m) -> p m t", t=PACK), h_bytes_raw[:].rearrange("p (m t) -> p m t", t=PACK)
        )
        h_bytes = keep.tile([P, C], U8, name="h_bytes", align_bytes=64)
        nc.gpsimd.memset(h_bytes[:].bitcast(I32), 0)
        for r, src in enumerate((0, 1, 16, 17)):
            nc.sync.dma_start(h_bytes[r:P:32, :].bitcast(I32), h_bytes_dealt[src:P:32, :].bitcast(I32))

        c_bytes = keep.tile([P, C], U8, name="c_bytes", tag="bytes_b", align_bytes=64)
        nc.vector.tensor_copy(c_bytes[:].rearrange("p (t m) -> p m t", t=PACK), x_bytes[:].indirect(ca_t[:]))
        h_codes_raw = keep.tile([P, C], U32, name="h_codes_raw", tag="window_bytes", align_bytes=64)
        nc.vector.tensor_copy(h_codes_raw[:], x_codes[:].indirect(hc_t[:]))
        h_codes = keep.tile([P, C], U32, name="h_codes", align_bytes=64)
        nc.vector.tensor_copy(
            h_codes[:].rearrange("p (t m) -> p m t", t=PACK), h_codes_raw[:].rearrange("p (m t) -> p m t", t=PACK)
        )
        c_codes = keep.tile([P, C], U32, name="c_codes", tag="codes_b", align_bytes=64)
        nc.vector.tensor_copy(c_codes[:].rearrange("p (t m) -> p m t", t=PACK), x_codes[:].indirect(ca_t[:]))

        z_bf = [
            keep.tile([P, HALF, PACK], BF16, name="z_bf%d" % h, tag=("window_codes", "window_bytes")[h], align_bytes=64)
            for h in range(2)
        ]
        for t in range(PACK - 1):
            for h in (1, 0):
                make_z(t, h)
        z_flat = keep.tile([P, HALF], BF16, name="z_flat", tag="sm0")
        nc.vector.scalar_tensor_tensor(z_flat[:], y_halves[3][1][1], gs_neg_half[:, 3:4], ds[3][:, HALF:S], MULT, ADD)
        nc.scalar.copy(z_bf[1][:, :, 3], z_flat[:])
        make_z(3, 0)

        a_first = [bank("a_ps0_%d" % h, 5 + h, HALF)[:] for h in range(2)]
        b_first = [bank("b_ps0_%d" % h, (7 + h) % 8, HALF)[:] for h in range(2)]
        for h, (cols, ent) in enumerate(HALVES):
            nc.vector.quantize_mx(z_codes[:, cols].bitcast(FP8X4), z_bytes[:, cols], z_bf[h][:].rearrange("p c t -> p (c t)"))
            mx(a_first[h], c_codes[:, 0:P], c_bytes[:, 0:P], z_codes[:, cols], z_bytes[:, cols])
            mx(b_first[h], h_codes[:, 0:P], h_bytes[:, 0:P], z_codes[:, cols], z_bytes[:, cols])
        a_banks, b_banks = [None], [None]
        for t in range(1, PACK):
            m = slice(t * P, (t + 1) * P)
            a_banks.append(bank("a_ps%d" % t, 2 * t - 1))
            mx(a_banks[t][:], c_codes[:, m], c_bytes[:, m], z_codes[:], z_bytes[:])
            b_banks.append(bank("b_ps%d" % t, 2 * t))
            mx(b_banks[t][:], h_codes[:, m], h_bytes[:, m], z_codes[:], z_bytes[:])

        out_rows = out.rearrange("(p t) n -> t p n", t=PACK)
        half_cols = [cols for cols, ent in HALVES]
        whole = slice(0, S)
        a_parts = [list(zip(half_cols, a_first))] + [[(whole, a_banks[t][:])] for t in range(1, PACK - 1)]
        b_parts = [list(zip(half_cols, b_first))] + [[(whole, b_banks[t][:])] for t in range(1, PACK - 1)]
        a_parts.append(list(zip(half_cols, halves_of(a_banks[PACK - 1]))))
        b_parts.append(list(zip(half_cols, halves_of(b_banks[PACK - 1]))))

        def first_windows():
            a_win = keep.tile([P, S], F32, name="a_win0")
            b_win = keep.tile([P, S], F32, name="b0_win")
            tops = keep.tile([P, 2], F32, name="b0_top", tag="b0_top")
            bias = keep.tile([P, 1], F32, name="b0_bias")
            for cols, a_part in a_parts[0]:
                nc.scalar.activation(a_win[:, cols], a_part, COPY, scale=0.125)
            for h, (cols, b_part) in enumerate(b_parts[0]):
                nc.vector.tensor_scalar(b_win[:, cols], b_part, 0.0625, None, MULT, MAX, accum_out=tops[:, h : h + 1])
            nc.gpsimd.tensor_scalar(bias[:], tops[:, 0:1], tops[:, 1:2], tau2_neg[:], MAX, MULT)
            return a_win, b_win, bias

        def windows(t):
            a_win = keep.tile([P, S], F32, name="a_win%d" % t)
            nc.vector.tensor_scalar(a_win[:], a_banks[t][:], 0.125, None, MULT)
            return (a_win,) + window_and_bias("b%d" % t, b_banks[t], 0.0625, tau2_t[:, t : t + 1])

        def finish(t, prod):
            res = keep.tile([P, S], F32, name="res%d" % t)
            for cols, b_part in b_parts[t]:
                nc.vector.scalar_tensor_tensor(res[:, cols], b_part, -0.03125, prod[:, cols], MULT, ADD)
            nc.sync.dma_start(out_rows[t], res[:])

        ready = [first_windows(), windows(1)]
        prods = []
        for t in range(PACK):
            a_win, b_win, bias = ready[t]
            looked = keep.tile([P, S], F32, name="looked%d" % t)
            diff = keep.tile([P, S], F32, name="diff%d" % t)
            ea2 = keep.tile([P, S], F32, name="ea2_%d" % t)
            for cols, ent in HALVES:
                nc.scalar.activation(looked[:, cols], a_win[:].indirect(n4_t[:, ent]), COPY)
            for cols, a_part in a_parts[t]:
                nc.vector.scalar_tensor_tensor(diff[:, cols], a_part, 0.125, looked[:, cols], MULT, SUB)
            for cols, ent in HALVES:
                nc.scalar.activation(ea2[:, cols], b_win[:].indirect(n3_t[:, ent]), EXP, bias=bias[:], scale=tau2_t[:, t : t + 1])
            if t > 0:
                finish(t - 1, prods[t - 1])
            prod = keep.tile([P, S], F32, name="prod%d" % t)
            if t + 1 < PACK:
                (nc.gpsimd if t < 2 else nc.vector).tensor_tensor(prod[:], diff[:], ea2[:], MULT)
                prods.append(prod)
            else:
                res = keep.tile([P, S], F32, name="res%d" % t)
                for cols, b_part in b_parts[t]:
                    nc.vector.tensor_tensor(prod[:, cols], diff[:, cols], ea2[:, cols], MULT)
                    nc.vector.scalar_tensor_tensor(res[:, cols], b_part, -0.03125, prod[:, cols], MULT, ADD)
                    nc.sync.dma_start(out_rows[t][:, cols], res[:, cols])
            if t + 2 < PACK:
                ready.append(windows(t + 2))
